import numpy as np
import ml_dtypes


def mxq(x, axis, fmt="e4m3"):
    dtype, down = {"e4m3": (ml_dtypes.float8_e4m3fn, 7), "e5m2": (ml_dtypes.float8_e5m2, 14)}[fmt]
    v = np.moveaxis(np.asarray(x, np.float32).astype(ml_dtypes.bfloat16).astype(np.float64), axis, -1)
    blocks = v.reshape(v.shape[:-1] + (-1, 32))
    amax = np.abs(blocks).max(-1, keepdims=True)
    byte = np.maximum(np.where(amax > 0, np.frexp(amax)[1] - 1 + 127, 0) - down, 1)
    scale = np.exp2(byte - 127.0)
    codes = (blocks / scale).astype(np.float32).astype(dtype).astype(np.float64)
    return np.moveaxis((codes * scale).reshape(v.shape), -1, axis)


WIDE = False


def mx_kscale(k):
    if not WIDE:
        return np.ones(k)
    levels = np.array([10, -10, 5, -5, 0])
    if k % 512:
        return np.exp2(np.random.permutation(np.resize(levels, k // 32))).repeat(32)
    a = np.empty((k // 512, 16))
    for p in range(k // 512):
        a[p, :8] = np.random.permutation(np.resize(levels, 8))
        for g in range(8):
            far = levels[np.abs(levels - a[p, g]) >= 10]
            a[p, g + 8] = far[np.random.randint(len(far))]
    return np.exp2(a.ravel()).repeat(32)


def f64(x):
    return np.asarray(x).astype(np.float64)


def striped(idx):
    return np.tile(idx.reshape(-1, 16).T, (8, 1)).astype(np.uint16)


def unstriped(offs):
    return offs[:16].T.reshape(-1).astype(np.int64)


def striped8(idx):
    return np.concatenate([x.reshape(-1, 16).T for x in idx]).astype(np.uint16)


def runs(offs, k):
    lists = np.stack([offs[16 * r : 16 * r + 16].T.reshape(-1) for r in range(8)]).astype(np.int64)
    return lists[np.arange(k) % 512 // 64]


def pack_weight(w):
    k, n = w.shape
    w = f64(np.asarray(w, np.float32).astype(ml_dtypes.bfloat16)).reshape(k // 32, 32, n)
    amax = np.abs(w).max(1)
    byte = np.clip(np.where(amax > 0, np.frexp(amax)[1] - 1 + 127 - 7, 1), 1, 254)
    scaled = (w * np.exp2(127.0 - byte)[:, None, :]).reshape(k, n).astype(np.float32)
    words = np.ascontiguousarray(scaled.reshape(k // 512, 128, 4, n).transpose(0, 1, 3, 2)).astype(ml_dtypes.float8_e4m3fn).view(np.uint8)
    return words, np.ascontiguousarray(byte.astype(np.uint8).reshape(k // 512, 16, n))


def unpack_weight(words, scales):
    g, p, n, _ = words.shape
    vals = np.ascontiguousarray(words).view(ml_dtypes.float8_e4m3fn).astype(np.float64) * np.repeat(np.exp2(scales.astype(np.float64) - 127.0), 8, axis=1)[..., None]
    return vals.transpose(0, 1, 3, 2).reshape(g * 512, n)


def sigmoid(v):
    return 1.0 / (1.0 + np.exp(-np.maximum(v, -700.0)))


K, T, S, N, G, H = 512, 1024, 256, 512, 2048, 512


def setup_inputs():
    n = np.random.standard_normal
    s = mx_kscale(K)[:, None]
    u = mx_kscale(K)
    packed_xT = pack_weight(n((K, T)) * s)
    packed_dT = pack_weight(n((K, G)) / s)
    packed_w1 = pack_weight(n((H, N)) / np.sqrt(2 * H) / u[:, None])
    packed_w2 = pack_weight(n((K, N)) / np.sqrt(2 * K) / s)
    return {
        "x_words": packed_xT[0],
        "x_scales": packed_xT[1],
        "d_words": packed_dT[0],
        "d_scales": packed_dT[1],
        "sl": np.random.uniform(1.0, 2.0, (H, 1)).astype(np.float32),
        "th": (0.5 * n((H, 1))).astype(np.float32),
        "gn": (np.random.uniform(0.5, 1.5, (H, 1)) * u[:, None]).astype(np.float32),
        "w1_words": packed_w1[0],
        "w1_scales": packed_w1[1],
        "w2_words": packed_w2[0],
        "w2_scales": packed_w2[1],
        "offs": striped(np.random.permutation(T)[:S]),
        "ci": striped(np.random.permutation(G)[:H]),
        "n1": striped8(np.stack([np.random.permutation(S) for _ in range(8)])),
        "n2": striped8(np.stack([np.random.permutation(S) for _ in range(8)])),
        "two": striped(np.random.permutation(T)[:S]),
        "n3": striped(np.random.permutation(S)),
    }


def reference(x_words, x_scales, d_words, d_scales, sl, th, gn, w1_words, w1_scales, w2_words, w2_scales, offs, ci, n1, n2, two, n3):
    d_ci = unpack_weight(d_words, d_scales)[:, unstriped(ci)]
    xq = unpack_weight(x_words, x_scales)[:, unstriped(offs)]
    s = 0.0625 * (d_ci.T @ xq)
    pa = s[np.arange(H)[:, None], runs(n1, H)]
    sg = sigmoid(f64(sl) * (s[np.arange(H)[:, None], runs(n2, H)] - f64(th)))
    z = f64(gn) * (pa + sg * (s - pa))
    x_two = unpack_weight(x_words, x_scales)[:, unstriped(two)]
    h = unpack_weight(w1_words, w1_scales).T @ mxq(z, 0, "e4m3") + unpack_weight(w2_words, w2_scales).T @ x_two
    ds = np.zeros((N, S))
    ds[:, unstriped(n3)] = h
    return h - ds

@@ -1,0 +1,185 @@
+from contextlib import ExitStack
+
+import concourse.mybir as mybir
+
+K, T, S, N, G, H = 512, 1024, 256, 512, 2048, 512
+FLOPS = 2 * K * H * S + 2 * H * N * S + 2 * K * N * S
+
+F32 = mybir.dt.float32
+BF16 = mybir.dt.bfloat16
+I32 = mybir.dt.int32
+U32 = mybir.dt.uint32
+U16 = mybir.dt.uint16
+U8 = mybir.dt.uint8
+FP8X4 = mybir.dt.float8_e4m3fn_x4
+ALU = mybir.AluOpType
+ACT = mybir.ActivationFunctionType
+
+P = 128
+PACK = 4
+QUADS = 4
+HALF = S // 2
+LIST_ROWS = 16
+D_ROW, X_ROW, W2_ROW, W1_ROW = 0, 4, 8, 12
+
+
+def load_words(queue, tile, words):
+    queue.dma_start(out=tile[:].bitcast(I32), in_=words[0].rearrange("p n t -> p (n t)").bitcast(I32))
+
+
+def load_scale_rows(queue, plane, scales, row0, q):
+    queue.dma_start(
+        out=plane[32 * q + row0 : 32 * q + row0 + 4, :].bitcast(I32),
+        in_=scales[0, 4 * q : 4 * q + 4, :].bitcast(I32),
+    )
+
+
+def tile_picked_dwmeblsendmx_none_p_kernel(
+    tc, x_words, x_scales, d_words, d_scales, sl, th, gn, w1_words, w1_scales, w2_words, w2_scales,
+    offs, ci, n1, n2, two, n3, out,
+):
+    nc = tc.nc
+    with ExitStack() as ctx:
+        lists = ctx.enter_context(tc.tile_pool(name="lists", bufs=1))
+        keep = ctx.enter_context(tc.tile_pool(name="keep", bufs=1))
+        psum = ctx.enter_context(tc.psum_pool(name="psum", bufs=1))
+
+        def list_tile(name, src):
+            t = lists.tile([P, src.shape[1]], U16, name=name + "_list")
+            nc.sync.dma_start(t[:], src)
+            return t
+
+        d_plane = keep.tile([P, G], U8, name="d_plane", align_bytes=64)
+        x_plane = keep.tile([P, T], U8, name="x_plane", align_bytes=64)
+        w_plane = keep.tile([P, N], U8, name="w_plane", align_bytes=64)
+        d_tab = keep.tile([P, G], U32, name="d_tab", align_bytes=64)
+        x_tab = keep.tile([P, T], U32, name="x_tab", align_bytes=64)
+        slope = keep.tile([P, PACK], F32, name="slope")
+        thresh = keep.tile([P, PACK], F32, name="thresh")
+        gain = keep.tile([P, PACK], F32, name="gain")
+        prod = keep.tile([P, PACK], F32, name="prod")
+        bias = keep.tile([P, PACK], F32, name="bias")
+
+        nc.gpsimd.memset(d_plane[:].bitcast(I32), 0)
+        nc.gpsimd.memset(x_plane[:].bitcast(I32), 0)
+        ci_t = list_tile("ci", ci)
+        offs_t = list_tile("offs", offs)
+        n2_t = list_tile("n2", n2)
+        n1_t = list_tile("n1", n1)
+        load_words(nc.sync, x_tab, x_words)
+        two_t = list_tile("two", two)
+        n3_t = list_tile("n3", n3)
+        load_words(nc.sync, d_tab, d_words)
+        for q in range(QUADS):
+            load_scale_rows(nc.scalar, d_plane, d_scales, D_ROW, q)
+        for q in range(QUADS):
+            load_scale_rows(nc.scalar if q < 3 else nc.gpsimd, x_plane, x_scales, X_ROW, q)
+        for tile, vec in ((slope, sl), (thresh, th), (gain, gn)):
+            nc.gpsimd.dma_start(out=tile[:], in_=vec.rearrange("(p t) o -> p (t o)", t=PACK))
+        nc.gpsimd.memset(w_plane[:].bitcast(I32), 0)
+
+        nc.gpsimd.tensor_tensor(prod[:], slope[:], thresh[:], ALU.mult)
+        nc.gpsimd.tensor_scalar(bias[:], prod[:], -1.0, 0.0, ALU.mult, ALU.add)
+
+        d_codes = keep.tile([P, H], U32, name="d_codes", align_bytes=64)
+        d_bytes = keep.tile([P, H], U8, name="d_bytes", align_bytes=64)
+        xq_codes = keep.tile([P, S], U32, name="xq_codes", align_bytes=64)
+        xq_bytes = keep.tile([P, S], U8, name="xq_bytes", align_bytes=64)
+
+        nc.vector.tensor_copy(xq_codes[:], x_tab[:].indirect(offs_t[:]))
+        nc.vector.tensor_copy(d_bytes[:].rearrange("p (t m) -> p m t", t=PACK), d_plane[:].indirect(ci_t[:]))
+        nc.vector.tensor_copy(xq_bytes[:], x_plane[:].indirect(offs_t[:]))
+        nc.vector.tensor_copy(d_codes[:].rearrange("p (t m) -> p m t", t=PACK), d_tab[:].indirect(ci_t[:]))
+
+        w2_codes = keep.tile([P, N], U32, name="w2_codes", tag="d_plane", align_bytes=64)
+        w1_codes = keep.tile([P, N], U32, name="w1_codes", tag="d_tab", align_bytes=64)
+        load_words(nc.sync, w2_codes, w2_words)
+        for q in range(QUADS):
+            load_scale_rows(nc.sync, w_plane, w2_scales, W2_ROW, q)
+        for q in range(QUADS):
+            load_scale_rows(nc.sync, w_plane, w1_scales, W1_ROW, q)
+        load_words(nc.sync, w1_codes, w1_words)
+
+        def half_of(list_t, a):
+            c = HALF // LIST_ROWS
+            return list_t[:, a * c : (a + 1) * c]
+
+        def gather_two(a):
+            codes = keep.tile([P, HALF], U32, name=f"two_codes{a}", align_bytes=64)
+            scales = keep.tile([P, HALF], U8, name=f"two_bytes{a}", align_bytes=64)
+            nc.vector.tensor_copy(codes[:], x_tab[:].indirect(half_of(two_t, a)))
+            nc.vector.tensor_copy(scales[:], x_plane[:].indirect(half_of(two_t, a)))
+            return codes, scales
+
+        two_ops = [gather_two(0)]
+
+        s_rows = []
+        for t in range(PACK):
+            cols = slice(P * t, P * (t + 1))
+            acc = psum.tile([P, S], F32, name=f"s_acc{t}", tag=f"bank{t}")
+            nc.tensor.matmul_mx(
+                out=acc[:], lhsT=d_codes[:, cols].bitcast(FP8X4), lhsT_scale=d_bytes[D_ROW:, cols],
+                rhs=xq_codes[:].bitcast(FP8X4), rhs_scale=xq_bytes[X_ROW:, :], start=True, stop=True,
+            )
+            s_t = keep.tile([P, S], F32, name=f"s{t}")
+            nc.vector.tensor_scalar(s_t[:], acc[:], 0.0625, None, ALU.mult)
+            s_rows.append(s_t)
+
+        h_rows = [keep.tile([P, S], F32, name=f"h{m}") for m in range(N // P)]
+        ds_rows = [keep.tile([P, S], F32, name=f"ds{m}") for m in range(N // P)]
+
+        for a in range(2):
+            cols = slice(a * HALF, (a + 1) * HALF)
+            z_rows = keep.tile([P, PACK, HALF], BF16, name=f"z_rows{a}", align_bytes=64)
+            for t in range(PACK):
+                sg = keep.tile([P, HALF], F32, name=f"sg{a}{t}", tag=f"sg{t}")
+                pa = keep.tile([P, HALF], F32, name=f"pa{a}{t}", tag=f"pa{t}")
+                nc.scalar.activation(
+                    out=sg[:], in_=s_rows[t][:].indirect(half_of(n2_t, a)), func=ACT.Sigmoid,
+                    scale=slope[:, t : t + 1], bias=bias[:, t : t + 1],
+                )
+                nc.scalar.activation(out=pa[:], in_=s_rows[t][:].indirect(half_of(n1_t, a)), func=ACT.Copy)
+                diff = keep.tile([P, HALF], F32, name=f"diff{a}{t}")
+                step = keep.tile([P, HALF], F32, name=f"step{a}{t}")
+                nc.vector.tensor_tensor(diff[:], s_rows[t][:, cols], pa[:], ALU.subtract)
+                nc.vector.scalar_tensor_tensor(step[:], diff[:], gain[:, t : t + 1], sg[:], ALU.mult, ALU.mult)
+                nc.vector.scalar_tensor_tensor(z_rows[:, t, :], pa[:], gain[:, t : t + 1], step[:], ALU.mult, ALU.add)
+
+            z_packed = keep.tile([P, HALF, PACK], BF16, name=f"z_packed{a}", align_bytes=64)
+            nc.vector.tensor_copy(
+                z_packed[:].rearrange("p (c i) t -> p c t i", i=4),
+                z_rows[:].rearrange("p t (c i) -> p c t i", i=4),
+            )
+            z_codes = keep.tile([P, HALF], U32, name=f"z_codes{a}", align_bytes=64)
+            z_bytes = keep.tile([P, HALF], U8, name=f"z_bytes{a}", align_bytes=64)
+            nc.vector.quantize_mx(
+                out=z_codes[:].bitcast(FP8X4), scales=z_bytes[:], in_=z_packed[:].rearrange("p j t -> p (j t)")
+            )
+            if a == 0:
+                two_ops.append(gather_two(1))
+
+            two_codes, two_bytes = two_ops[a]
+            accs = []
+            for m in range(N // P):
+                rows = slice(P * m, P * (m + 1))
+                acc = psum.tile([P, HALF], F32, name=f"h_acc{a}{m}", tag=f"bank{(m + 4 * (1 - a))}")
+                nc.tensor.matmul_mx(
+                    out=acc[:], lhsT=w2_codes[:, rows].bitcast(FP8X4), lhsT_scale=w_plane[W2_ROW:, rows],
+                    rhs=two_codes[:].bitcast(FP8X4), rhs_scale=two_bytes[X_ROW:, :], start=True, stop=False,
+                )
+                accs.append(acc)
+            for m in range(N // P):
+                rows = slice(P * m, P * (m + 1))
+                nc.tensor.matmul_mx(
+                    out=accs[m][:], lhsT=w1_codes[:, rows].bitcast(FP8X4), lhsT_scale=w_plane[W1_ROW:, rows],
+                    rhs=z_codes[:].bitcast(FP8X4), rhs_scale=z_bytes[:], start=False, stop=True,
+                )
+                nc.vector.tensor_copy(h_rows[m][:, cols], accs[m][:])
+                nc.scalar.activation(
+                    out=ds_rows[m][:].indirect(half_of(n3_t, a)), in_=h_rows[m][:, cols], func=ACT.Copy
+                )
+
+        for m in range(N // P):
+            res = keep.tile([P, S], F32, name=f"res{m}")
+            nc.vector.tensor_tensor(res[:], h_rows[m][:], ds_rows[m][:], ALU.subtract)
+            nc.sync.dma_start(out=out[P * m : P * (m + 1), :], in_=res[:])

@@ -19,19 +19,25 @@ P = 128
 PACK = 4
 QUADS = 4
 HALF = S // 2
-LIST_ROWS = 16
-D_ROW, X_ROW, W2_ROW, W1_ROW = 0, 4, 8, 12
+LIST_COLS = HALF // 16
+HALF_BYTES = 4 * HALF
+D_FIRST, X_FIRST, W2_FIRST, W1_FIRST = 0, 4, 8, 12
+OUT_GROUPS = (range(0, 1), range(1, N // P))
 
 
 def load_words(queue, tile, words):
-    queue.dma_start(out=tile[:].bitcast(I32), in_=words[0].rearrange("p n t -> p (n t)").bitcast(I32))
+    queue.dma_start(out=tile[:].bitcast(I32), in_=words[0].rearrange("p n r -> p (n r)").bitcast(I32))
 
 
-def load_scale_rows(queue, plane, scales, row0, q):
+def load_scale_rows(queue, plane, scales, first, q):
     queue.dma_start(
-        out=plane[32 * q + row0 : 32 * q + row0 + 4, :].bitcast(I32),
+        out=plane[32 * q + first : 32 * q + first + 4, :].bitcast(I32),
         in_=scales[0, 4 * q : 4 * q + 4, :].bitcast(I32),
     )
+
+
+def load_column(queue, tile, vec):
+    queue.dma_start(out=tile[:], in_=vec.rearrange("(p t) o -> p (t o)", t=PACK))
 
 
 def tile_picked_dwmeblsendmx_none_p_kernel(
@@ -42,144 +48,157 @@ def tile_picked_dwmeblsendmx_none_p_kernel(
     with ExitStack() as ctx:
         lists = ctx.enter_context(tc.tile_pool(name="lists", bufs=1))
         keep = ctx.enter_context(tc.tile_pool(name="keep", bufs=1))
+        on_d = ctx.enter_context(tc.tile_pool(name="on_d", bufs=1))
+        on_x = ctx.enter_context(tc.tile_pool(name="on_x", bufs=1))
+        on_z = ctx.enter_context(tc.tile_pool(name="on_z", bufs=1))
         psum = ctx.enter_context(tc.psum_pool(name="psum", bufs=1))
 
-        def list_tile(name, src):
-            t = lists.tile([P, src.shape[1]], U16, name=name + "_list")
-            nc.sync.dma_start(t[:], src)
-            return t
+        def load_list(name, src):
+            tile = lists.tile([P, src.shape[1]], U16, name=name + "_list")
+            nc.sync.dma_start(tile[:], src)
+            return tile
+
+        def half_of(list_tile, a):
+            return list_tile[:, a * LIST_COLS : (a + 1) * LIST_COLS]
 
         d_plane = keep.tile([P, G], U8, name="d_plane", align_bytes=64)
         x_plane = keep.tile([P, T], U8, name="x_plane", align_bytes=64)
         w_plane = keep.tile([P, N], U8, name="w_plane", align_bytes=64)
-        d_tab = keep.tile([P, G], U32, name="d_tab", align_bytes=64)
-        x_tab = keep.tile([P, T], U32, name="x_tab", align_bytes=64)
+        d_table = on_d.tile([P, G], U32, name="d_table", align_bytes=64, offset=0)
+        x_table = on_x.tile([P, T], U32, name="x_table", align_bytes=64, offset=0)
+        w1_codes = keep.tile([P, N], U32, name="w1_codes", align_bytes=64)
+        w2_codes = keep.tile([P, N], U32, name="w2_codes", align_bytes=64)
         slope = keep.tile([P, PACK], F32, name="slope")
         thresh = keep.tile([P, PACK], F32, name="thresh")
         gain = keep.tile([P, PACK], F32, name="gain")
-        prod = keep.tile([P, PACK], F32, name="prod")
-        bias = keep.tile([P, PACK], F32, name="bias")
 
-        nc.gpsimd.memset(d_plane[:].bitcast(I32), 0)
-        nc.gpsimd.memset(x_plane[:].bitcast(I32), 0)
-        ci_t = list_tile("ci", ci)
-        offs_t = list_tile("offs", offs)
-        n2_t = list_tile("n2", n2)
-        n1_t = list_tile("n1", n1)
-        load_words(nc.sync, x_tab, x_words)
-        two_t = list_tile("two", two)
-        n3_t = list_tile("n3", n3)
-        load_words(nc.sync, d_tab, d_words)
-        for q in range(QUADS):
-            load_scale_rows(nc.scalar, d_plane, d_scales, D_ROW, q)
-        for q in range(QUADS):
-            load_scale_rows(nc.scalar if q < 3 else nc.gpsimd, x_plane, x_scales, X_ROW, q)
-        for tile, vec in ((slope, sl), (thresh, th), (gain, gn)):
-            nc.gpsimd.dma_start(out=tile[:], in_=vec.rearrange("(p t) o -> p (t o)", t=PACK))
+        nc.vector.memset(d_plane[:].bitcast(I32), 0)
+        nc.vector.memset(x_plane[:].bitcast(I32), 0)
         nc.gpsimd.memset(w_plane[:].bitcast(I32), 0)
 
-        nc.gpsimd.tensor_tensor(prod[:], slope[:], thresh[:], ALU.mult)
-        nc.gpsimd.tensor_scalar(bias[:], prod[:], -1.0, 0.0, ALU.mult, ALU.add)
+        ci_list = load_list("ci", ci)
+        offs_list = load_list("offs", offs)
+        for q in range(QUADS):
+            load_scale_rows(nc.scalar if q < QUADS // 2 else nc.sync, d_plane, d_scales, D_FIRST, q)
+        load_words(nc.sync, d_table, d_words)
+        load_words(nc.sync, x_table, x_words)
+        for q in range(QUADS):
+            load_scale_rows(nc.scalar, x_plane, x_scales, X_FIRST, q)
+        n1_list = load_list("n1", n1)
+        n2_list = load_list("n2", n2)
+        two_list = load_list("two", two)
+        load_words(nc.sync, w2_codes, w2_words)
+        load_words(nc.sync, w1_codes, w1_words)
+        for tile, vec in ((thresh, th), (slope, sl), (gain, gn)):
+            load_column(nc.gpsimd, tile, vec)
+        for q in range(QUADS):
+            load_scale_rows(nc.sync, w_plane, w2_scales, W2_FIRST, q)
+            load_scale_rows(nc.gpsimd, w_plane, w1_scales, W1_FIRST, q)
+        n3_list = load_list("n3", n3)
+
+        minus_thresh = keep.tile([P, PACK], F32, name="minus_thresh")
+        nc.scalar.activation(out=minus_thresh[:], in_=thresh[:], func=ACT.Copy, scale=-1.0)
 
         d_codes = keep.tile([P, H], U32, name="d_codes", align_bytes=64)
         d_bytes = keep.tile([P, H], U8, name="d_bytes", align_bytes=64)
-        xq_codes = keep.tile([P, S], U32, name="xq_codes", align_bytes=64)
         xq_bytes = keep.tile([P, S], U8, name="xq_bytes", align_bytes=64)
-
-        nc.vector.tensor_copy(xq_codes[:], x_tab[:].indirect(offs_t[:]))
-        nc.vector.tensor_copy(d_bytes[:].rearrange("p (t m) -> p m t", t=PACK), d_plane[:].indirect(ci_t[:]))
-        nc.vector.tensor_copy(xq_bytes[:], x_plane[:].indirect(offs_t[:]))
-        nc.vector.tensor_copy(d_codes[:].rearrange("p (t m) -> p m t", t=PACK), d_tab[:].indirect(ci_t[:]))
-
-        w2_codes = keep.tile([P, N], U32, name="w2_codes", tag="d_plane", align_bytes=64)
-        w1_codes = keep.tile([P, N], U32, name="w1_codes", tag="d_tab", align_bytes=64)
-        load_words(nc.sync, w2_codes, w2_words)
-        for q in range(QUADS):
-            load_scale_rows(nc.sync, w_plane, w2_scales, W2_ROW, q)
-        for q in range(QUADS):
-            load_scale_rows(nc.sync, w_plane, w1_scales, W1_ROW, q)
-        load_words(nc.sync, w1_codes, w1_words)
-
-        def half_of(list_t, a):
-            c = HALF // LIST_ROWS
-            return list_t[:, a * c : (a + 1) * c]
-
-        def gather_two(a):
-            codes = keep.tile([P, HALF], U32, name=f"two_codes{a}", align_bytes=64)
-            scales = keep.tile([P, HALF], U8, name=f"two_bytes{a}", align_bytes=64)
-            nc.vector.tensor_copy(codes[:], x_tab[:].indirect(half_of(two_t, a)))
-            nc.vector.tensor_copy(scales[:], x_plane[:].indirect(half_of(two_t, a)))
-            return codes, scales
-
-        two_ops = [gather_two(0)]
+        nc.vector.tensor_copy(d_bytes[:].rearrange("p (t m) -> p m t", t=PACK), d_plane[:].indirect(ci_list[:]))
+        nc.vector.tensor_copy(xq_bytes[:], x_plane[:].indirect(offs_list[:]))
+        nc.vector.tensor_copy(d_codes[:].rearrange("p (t m) -> p m t", t=PACK), d_table[:].indirect(ci_list[:]))
+        xq_codes = on_d.tile([P, S], U32, name="xq_codes", align_bytes=64, offset=0)
+        two_bytes = on_d.tile([P, S], U8, name="two_bytes", align_bytes=64, offset=4 * S)
+        bias = on_d.tile([P, PACK], F32, name="bias", align_bytes=64, offset=5 * S)
+        nc.vector.tensor_copy(xq_codes[:], x_table[:].indirect(offs_list[:]))
+        nc.vector.tensor_tensor(bias[:], slope[:], minus_thresh[:], ALU.mult)
+        nc.vector.tensor_copy(two_bytes[:], x_plane[:].indirect(two_list[:]))
 
         s_rows = []
         for t in range(PACK):
             cols = slice(P * t, P * (t + 1))
-            acc = psum.tile([P, S], F32, name=f"s_acc{t}", tag=f"bank{t}")
+            s_acc = psum.tile([P, S], F32, name=f"s_acc{t}")
             nc.tensor.matmul_mx(
-                out=acc[:], lhsT=d_codes[:, cols].bitcast(FP8X4), lhsT_scale=d_bytes[D_ROW:, cols],
-                rhs=xq_codes[:].bitcast(FP8X4), rhs_scale=xq_bytes[X_ROW:, :], start=True, stop=True,
+                out=s_acc[:], lhsT=d_codes[:, cols].bitcast(FP8X4), lhsT_scale=d_bytes[D_FIRST:, cols],
+                rhs=xq_codes[:].bitcast(FP8X4), rhs_scale=xq_bytes[X_FIRST:, :], start=True, stop=True,
             )
-            s_t = keep.tile([P, S], F32, name=f"s{t}")
-            nc.vector.tensor_scalar(s_t[:], acc[:], 0.0625, None, ALU.mult)
-            s_rows.append(s_t)
+            s_row = keep.tile([P, S], F32, name=f"s{t}")
+            if t == 0:
+                nc.scalar.activation(out=s_row[:], in_=s_acc[:], func=ACT.Copy, scale=0.0625)
+            else:
+                nc.vector.tensor_scalar(s_row[:], s_acc[:], 0.0625, None, ALU.mult)
+            s_rows.append(s_row)
 
-        h_rows = [keep.tile([P, S], F32, name=f"h{m}") for m in range(N // P)]
+        two_codes = keep.tile([P, S], U32, name="two_codes", tag="d_codes", align_bytes=64)
+        nc.vector.tensor_copy(two_codes[:], x_table[:].indirect(two_list[:]))
+
+        h_all = keep.tile([P, N // P, S], F32, name="h_all")
         ds_rows = [keep.tile([P, S], F32, name=f"ds{m}") for m in range(N // P)]
 
         for a in range(2):
             cols = slice(a * HALF, (a + 1) * HALF)
-            z_rows = keep.tile([P, PACK, HALF], BF16, name=f"z_rows{a}", align_bytes=64)
+            if a == 0:
+                z_rows = on_z.tile([P, PACK, HALF], BF16, name="z_rows0", align_bytes=64, offset=0)
+                z_woven = on_z.tile([P, HALF, PACK], BF16, name="z_woven0", align_bytes=64, offset=2 * HALF_BYTES)
+                z_codes = on_z.tile([P, HALF], U32, name="z_codes0", align_bytes=64, offset=4 * HALF_BYTES)
+            else:
+                z_rows = keep.tile([P, PACK, HALF], BF16, name="z_rows1", align_bytes=64)
+                z_woven = keep.tile([P, HALF, PACK], BF16, name="z_woven1", align_bytes=64)
+                z_codes = keep.tile([P, HALF], U32, name="z_codes1", align_bytes=64)
+            z_bytes = keep.tile([P, HALF], U8, name=f"z_bytes{a}", align_bytes=64)
+
             for t in range(PACK):
-                sg = keep.tile([P, HALF], F32, name=f"sg{a}{t}", tag=f"sg{t}")
-                pa = keep.tile([P, HALF], F32, name=f"pa{a}{t}", tag=f"pa{t}")
+                if a == 0:
+                    pa = keep.tile([P, HALF], F32, name=f"pa0{t}")
+                    sg = keep.tile([P, HALF], F32, name=f"sg0{t}")
+                    diff = keep.tile([P, HALF], F32, name=f"diff0{t}")
+                else:
+                    pa = on_x.tile([P, HALF], F32, name=f"pa1{t}", offset=2 * t * HALF_BYTES)
+                    sg = on_x.tile([P, HALF], F32, name=f"sg1{t}", offset=(2 * t + 1) * HALF_BYTES)
+                    diff = on_z.tile([P, HALF], F32, name=f"diff1{t}", offset=(t + t // 3) * HALF_BYTES)
+                step = keep.tile([P, HALF], F32, name=f"step{a}{t}")
+                nc.scalar.activation(out=pa[:], in_=s_rows[t][:].indirect(half_of(n1_list, a)), func=ACT.Copy)
                 nc.scalar.activation(
-                    out=sg[:], in_=s_rows[t][:].indirect(half_of(n2_t, a)), func=ACT.Sigmoid,
+                    out=sg[:], in_=s_rows[t][:].indirect(half_of(n2_list, a)), func=ACT.Sigmoid,
                     scale=slope[:, t : t + 1], bias=bias[:, t : t + 1],
                 )
-                nc.scalar.activation(out=pa[:], in_=s_rows[t][:].indirect(half_of(n1_t, a)), func=ACT.Copy)
-                diff = keep.tile([P, HALF], F32, name=f"diff{a}{t}")
-                step = keep.tile([P, HALF], F32, name=f"step{a}{t}")
                 nc.vector.tensor_tensor(diff[:], s_rows[t][:, cols], pa[:], ALU.subtract)
                 nc.vector.scalar_tensor_tensor(step[:], diff[:], gain[:, t : t + 1], sg[:], ALU.mult, ALU.mult)
-                nc.vector.scalar_tensor_tensor(z_rows[:, t, :], pa[:], gain[:, t : t + 1], step[:], ALU.mult, ALU.add)
+                nc.vector.scalar_tensor_tensor(
+                    z_rows[:, t, :], pa[:], gain[:, t : t + 1], step[:], ALU.mult, ALU.add
+                )
 
-            z_packed = keep.tile([P, HALF, PACK], BF16, name=f"z_packed{a}", align_bytes=64)
             nc.vector.tensor_copy(
-                z_packed[:].rearrange("p (c i) t -> p c t i", i=4),
-                z_rows[:].rearrange("p t (c i) -> p c t i", i=4),
+                z_woven[:].rearrange("p (c i) t -> p c t i", i=4), z_rows[:].rearrange("p t (c i) -> p c t i", i=4)
             )
-            z_codes = keep.tile([P, HALF], U32, name=f"z_codes{a}", align_bytes=64)
-            z_bytes = keep.tile([P, HALF], U8, name=f"z_bytes{a}", align_bytes=64)
             nc.vector.quantize_mx(
-                out=z_codes[:].bitcast(FP8X4), scales=z_bytes[:], in_=z_packed[:].rearrange("p j t -> p (j t)")
+                out=z_codes[:].bitcast(FP8X4), scales=z_bytes[:], in_=z_woven[:].rearrange("p j t -> p (j t)")
             )
-            if a == 0:
-                two_ops.append(gather_two(1))
 
-            two_codes, two_bytes = two_ops[a]
-            accs = []
-            for m in range(N // P):
-                rows = slice(P * m, P * (m + 1))
-                acc = psum.tile([P, HALF], F32, name=f"h_acc{a}{m}", tag=f"bank{(m + 4 * (1 - a))}")
-                nc.tensor.matmul_mx(
-                    out=acc[:], lhsT=w2_codes[:, rows].bitcast(FP8X4), lhsT_scale=w_plane[W2_ROW:, rows],
-                    rhs=two_codes[:].bitcast(FP8X4), rhs_scale=two_bytes[X_ROW:, :], start=True, stop=False,
-                )
-                accs.append(acc)
-            for m in range(N // P):
-                rows = slice(P * m, P * (m + 1))
-                nc.tensor.matmul_mx(
-                    out=accs[m][:], lhsT=w1_codes[:, rows].bitcast(FP8X4), lhsT_scale=w_plane[W1_ROW:, rows],
-                    rhs=z_codes[:].bitcast(FP8X4), rhs_scale=z_bytes[:], start=False, stop=True,
-                )
-                nc.vector.tensor_copy(h_rows[m][:, cols], accs[m][:])
-                nc.scalar.activation(
-                    out=ds_rows[m][:].indirect(half_of(n3_t, a)), in_=h_rows[m][:, cols], func=ACT.Copy
-                )
+            h_accs = [psum.tile([P, len(ms), HALF], F32, name=f"h_acc{a}{ms[0]}") for ms in OUT_GROUPS]
+            for h_acc, ms in zip(h_accs, OUT_GROUPS):
+                for m in ms:
+                    rows = slice(P * m, P * (m + 1))
+                    nc.tensor.matmul_mx(
+                        out=h_acc[:, m - ms[0], :],
+                        lhsT=w2_codes[:, rows].bitcast(FP8X4), lhsT_scale=w_plane[W2_FIRST:, rows],
+                        rhs=two_codes[:, cols].bitcast(FP8X4), rhs_scale=two_bytes[X_FIRST:, cols],
+                        start=(m == ms[0]), stop=False,
+                    )
+            for h_acc, ms in zip(h_accs, OUT_GROUPS):
+                for m in ms:
+                    rows = slice(P * m, P * (m + 1))
+                    nc.tensor.matmul_mx(
+                        out=h_acc[:, m - ms[0], :],
+                        lhsT=w1_codes[:, rows].bitcast(FP8X4), lhsT_scale=w_plane[W1_FIRST:, rows],
+                        rhs=z_codes[:].bitcast(FP8X4), rhs_scale=z_bytes[:],
+                        start=False, stop=(m == ms[-1]),
+                    )
+                nc.vector.tensor_copy(h_all[:, ms[0] : ms[-1] + 1, cols], h_acc[:])
+                for m in ms:
+                    nc.scalar.activation(
+                        out=ds_rows[m][:].indirect(half_of(n3_list, a)), in_=h_all[:, m, cols], func=ACT.Copy
+                    )
 
         for m in range(N // P):
             res = keep.tile([P, S], F32, name=f"res{m}")
-            nc.vector.tensor_tensor(res[:], h_rows[m][:], ds_rows[m][:], ALU.subtract)
+            nc.vector.tensor_tensor(res[:], h_all[:, m, :], ds_rows[m][:], ALU.subtract)
             nc.sync.dma_start(out=out[P * m : P * (m + 1), :], in_=res[:])

@@ -72,7 +72,8 @@ def tile_picked_dwmeblsendmx_none_p_kernel(
         thresh = keep.tile([P, PACK], F32, name="thresh")
         gain = keep.tile([P, PACK], F32, name="gain")
 
-        nc.vector.memset(d_plane[:].bitcast(I32), 0)
+        nc.vector.memset(d_plane[:, : G // 2].bitcast(I32), 0)
+        nc.gpsimd.memset(d_plane[:, G // 2 :].bitcast(I32), 0)
         nc.vector.memset(x_plane[:].bitcast(I32), 0)
         nc.gpsimd.memset(w_plane[:].bitcast(I32), 0)
 
@@ -81,11 +82,11 @@ def tile_picked_dwmeblsendmx_none_p_kernel(
         for q in range(QUADS):
             load_scale_rows(nc.scalar if q < QUADS // 2 else nc.sync, d_plane, d_scales, D_FIRST, q)
         load_words(nc.sync, d_table, d_words)
-        load_words(nc.sync, x_table, x_words)
         for q in range(QUADS):
-            load_scale_rows(nc.scalar, x_plane, x_scales, X_FIRST, q)
+            load_scale_rows(nc.scalar if q < QUADS - 1 else nc.gpsimd, x_plane, x_scales, X_FIRST, q)
         n1_list = load_list("n1", n1)
         n2_list = load_list("n2", n2)
+        load_words(nc.sync, x_table, x_words)
         two_list = load_list("two", two)
         load_words(nc.sync, w2_codes, w2_words)
         load_words(nc.sync, w1_codes, w1_words)
@@ -93,7 +94,7 @@ def tile_picked_dwmeblsendmx_none_p_kernel(
             load_column(nc.gpsimd, tile, vec)
         for q in range(QUADS):
             load_scale_rows(nc.sync, w_plane, w2_scales, W2_FIRST, q)
-            load_scale_rows(nc.gpsimd, w_plane, w1_scales, W1_FIRST, q)
+            load_scale_rows(nc.gpsimd if q < QUADS - 1 else nc.sync, w_plane, w1_scales, W1_FIRST, q)
         n3_list = load_list("n3", n3)
 
         minus_thresh = keep.tile([P, PACK], F32, name="minus_thresh")
@@ -101,14 +102,14 @@ def tile_picked_dwmeblsendmx_none_p_kernel(
 
         d_codes = keep.tile([P, H], U32, name="d_codes", align_bytes=64)
         d_bytes = keep.tile([P, H], U8, name="d_bytes", align_bytes=64)
-        xq_bytes = keep.tile([P, S], U8, name="xq_bytes", align_bytes=64)
         nc.vector.tensor_copy(d_bytes[:].rearrange("p (t m) -> p m t", t=PACK), d_plane[:].indirect(ci_list[:]))
-        nc.vector.tensor_copy(xq_bytes[:], x_plane[:].indirect(offs_list[:]))
         nc.vector.tensor_copy(d_codes[:].rearrange("p (t m) -> p m t", t=PACK), d_table[:].indirect(ci_list[:]))
         xq_codes = on_d.tile([P, S], U32, name="xq_codes", align_bytes=64, offset=0)
-        two_bytes = on_d.tile([P, S], U8, name="two_bytes", align_bytes=64, offset=4 * S)
-        bias = on_d.tile([P, PACK], F32, name="bias", align_bytes=64, offset=5 * S)
+        xq_bytes = on_d.tile([P, S], U8, name="xq_bytes", align_bytes=64, offset=4 * S)
+        two_bytes = on_d.tile([P, S], U8, name="two_bytes", align_bytes=64, offset=5 * S)
+        bias = on_d.tile([P, PACK], F32, name="bias", align_bytes=64, offset=6 * S)
         nc.vector.tensor_copy(xq_codes[:], x_table[:].indirect(offs_list[:]))
+        nc.vector.tensor_copy(xq_bytes[:], x_plane[:].indirect(offs_list[:]))
         nc.vector.tensor_tensor(bias[:], slope[:], minus_thresh[:], ALU.mult)
         nc.vector.tensor_copy(two_bytes[:], x_plane[:].indirect(two_list[:]))
 
@@ -133,70 +134,124 @@ def tile_picked_dwmeblsendmx_none_p_kernel(
         h_all = keep.tile([P, N // P, S], F32, name="h_all")
         ds_rows = [keep.tile([P, S], F32, name=f"ds{m}") for m in range(N // P)]
 
-        for a in range(2):
-            cols = slice(a * HALF, (a + 1) * HALF)
+        halves = [slice(a * HALF, (a + 1) * HALF) for a in range(2)]
+
+        z_rows = [
+            on_z.tile([P, PACK, HALF], BF16, name="z_rows0", align_bytes=64, offset=0),
+            keep.tile([P, PACK, HALF], BF16, name="z_rows1", align_bytes=64),
+        ]
+        z_woven = [
+            on_z.tile([P, HALF, PACK], BF16, name="z_woven0", align_bytes=64, offset=2 * HALF_BYTES),
+            keep.tile([P, HALF, PACK], BF16, name="z_woven1", align_bytes=64),
+        ]
+        z_codes = [
+            on_z.tile([P, HALF], U32, name="z_codes0", align_bytes=64, offset=4 * HALF_BYTES),
+            keep.tile([P, HALF], U32, name="z_codes1", align_bytes=64),
+        ]
+        z_bytes = [keep.tile([P, HALF], U8, name=f"z_bytes{a}", align_bytes=64) for a in range(2)]
+        pa, sg, diff, step = {}, {}, {}, {}
+
+        def fetch(a, t):
             if a == 0:
-                z_rows = on_z.tile([P, PACK, HALF], BF16, name="z_rows0", align_bytes=64, offset=0)
-                z_woven = on_z.tile([P, HALF, PACK], BF16, name="z_woven0", align_bytes=64, offset=2 * HALF_BYTES)
-                z_codes = on_z.tile([P, HALF], U32, name="z_codes0", align_bytes=64, offset=4 * HALF_BYTES)
+                pa[a, t] = keep.tile([P, HALF], F32, name=f"pa0{t}")
+                sg[a, t] = keep.tile([P, HALF], F32, name=f"sg0{t}")
             else:
-                z_rows = keep.tile([P, PACK, HALF], BF16, name="z_rows1", align_bytes=64)
-                z_woven = keep.tile([P, HALF, PACK], BF16, name="z_woven1", align_bytes=64)
-                z_codes = keep.tile([P, HALF], U32, name="z_codes1", align_bytes=64)
-            z_bytes = keep.tile([P, HALF], U8, name=f"z_bytes{a}", align_bytes=64)
+                pa[a, t] = on_x.tile([P, HALF], F32, name=f"pa1{t}", offset=2 * t * HALF_BYTES)
+                sg[a, t] = on_x.tile([P, HALF], F32, name=f"sg1{t}", offset=(2 * t + 1) * HALF_BYTES)
+            nc.scalar.activation(out=pa[a, t][:], in_=s_rows[t][:].indirect(half_of(n1_list, a)), func=ACT.Copy)
+            nc.scalar.activation(
+                out=sg[a, t][:], in_=s_rows[t][:].indirect(half_of(n2_list, a)), func=ACT.Sigmoid,
+                scale=slope[:, t : t + 1], bias=bias[:, t : t + 1],
+            )
 
-            for t in range(PACK):
-                if a == 0:
-                    pa = keep.tile([P, HALF], F32, name=f"pa0{t}")
-                    sg = keep.tile([P, HALF], F32, name=f"sg0{t}")
-                    diff = keep.tile([P, HALF], F32, name=f"diff0{t}")
-                else:
-                    pa = on_x.tile([P, HALF], F32, name=f"pa1{t}", offset=2 * t * HALF_BYTES)
-                    sg = on_x.tile([P, HALF], F32, name=f"sg1{t}", offset=(2 * t + 1) * HALF_BYTES)
-                    diff = on_z.tile([P, HALF], F32, name=f"diff1{t}", offset=(t + t // 3) * HALF_BYTES)
-                step = keep.tile([P, HALF], F32, name=f"step{a}{t}")
-                nc.scalar.activation(out=pa[:], in_=s_rows[t][:].indirect(half_of(n1_list, a)), func=ACT.Copy)
-                nc.scalar.activation(
-                    out=sg[:], in_=s_rows[t][:].indirect(half_of(n2_list, a)), func=ACT.Sigmoid,
-                    scale=slope[:, t : t + 1], bias=bias[:, t : t + 1],
-                )
-                nc.vector.tensor_tensor(diff[:], s_rows[t][:, cols], pa[:], ALU.subtract)
-                nc.vector.scalar_tensor_tensor(step[:], diff[:], gain[:, t : t + 1], sg[:], ALU.mult, ALU.mult)
-                nc.vector.scalar_tensor_tensor(
-                    z_rows[:, t, :], pa[:], gain[:, t : t + 1], step[:], ALU.mult, ALU.add
-                )
+        def subtract(a, t):
+            if a == 0:
+                diff[a, t] = keep.tile([P, HALF], F32, name=f"diff0{t}")
+            elif t == 0:
+                diff[a, t] = keep.tile([P, HALF], F32, name="diff10", tag=f"diff0{PACK - 1}")
+            else:
+                diff[a, t] = on_z.tile([P, HALF], F32, name=f"diff1{t}", offset=2 * (t - 1) * HALF_BYTES)
+            nc.vector.tensor_tensor(diff[a, t][:], s_rows[t][:, halves[a]], pa[a, t][:], ALU.subtract)
 
+        def weigh(a, t):
+            step[a, t] = keep.tile([P, HALF], F32, name=f"step{a}{t}")
+            nc.vector.scalar_tensor_tensor(
+                step[a, t][:], diff[a, t][:], gain[:, t : t + 1], sg[a, t][:], ALU.mult, ALU.mult
+            )
+
+        def join(a, t):
+            nc.vector.scalar_tensor_tensor(
+                z_rows[a][:, t, :], pa[a, t][:], gain[:, t : t + 1], step[a, t][:], ALU.mult, ALU.add
+            )
+
+        def weave(a):
             nc.vector.tensor_copy(
-                z_woven[:].rearrange("p (c i) t -> p c t i", i=4), z_rows[:].rearrange("p t (c i) -> p c t i", i=4)
-            )
-            nc.vector.quantize_mx(
-                out=z_codes[:].bitcast(FP8X4), scales=z_bytes[:], in_=z_woven[:].rearrange("p j t -> p (j t)")
+                z_woven[a][:].rearrange("p (c i) t -> p c t i", i=4),
+                z_rows[a][:].rearrange("p t (c i) -> p c t i", i=4),
             )
 
+        def quantise(a):
+            nc.vector.quantize_mx(
+                out=z_codes[a][:].bitcast(FP8X4), scales=z_bytes[a][:],
+                in_=z_woven[a][:].rearrange("p j t -> p (j t)"),
+            )
+
+        def multiply(a):
             h_accs = [psum.tile([P, len(ms), HALF], F32, name=f"h_acc{a}{ms[0]}") for ms in OUT_GROUPS]
+            operands = (
+                (w2_codes, W2_FIRST, two_codes[:, halves[a]], two_bytes[X_FIRST:, halves[a]]),
+                (w1_codes, W1_FIRST, z_codes[a][:], z_bytes[a][:]),
+            )
+            for k, (w_codes, w_first, codes, scale_bytes) in enumerate(operands):
+                for h_acc, ms in zip(h_accs, OUT_GROUPS):
+                    for m in ms:
+                        rows = slice(P * m, P * (m + 1))
+                        nc.tensor.matmul_mx(
+                            out=h_acc[:, m - ms[0], :],
+                            lhsT=w_codes[:, rows].bitcast(FP8X4), lhsT_scale=w_plane[w_first:, rows],
+                            rhs=codes.bitcast(FP8X4), rhs_scale=scale_bytes,
+                            start=(k == 0 and m == ms[0]), stop=(k == 1 and m == ms[-1]),
+                        )
+            return h_accs
+
+        def send(a, h_accs):
             for h_acc, ms in zip(h_accs, OUT_GROUPS):
-                for m in ms:
-                    rows = slice(P * m, P * (m + 1))
-                    nc.tensor.matmul_mx(
-                        out=h_acc[:, m - ms[0], :],
-                        lhsT=w2_codes[:, rows].bitcast(FP8X4), lhsT_scale=w_plane[W2_FIRST:, rows],
-                        rhs=two_codes[:, cols].bitcast(FP8X4), rhs_scale=two_bytes[X_FIRST:, cols],
-                        start=(m == ms[0]), stop=False,
-                    )
-            for h_acc, ms in zip(h_accs, OUT_GROUPS):
-                for m in ms:
-                    rows = slice(P * m, P * (m + 1))
-                    nc.tensor.matmul_mx(
-                        out=h_acc[:, m - ms[0], :],
-                        lhsT=w1_codes[:, rows].bitcast(FP8X4), lhsT_scale=w_plane[W1_FIRST:, rows],
-                        rhs=z_codes[:].bitcast(FP8X4), rhs_scale=z_bytes[:],
-                        start=False, stop=(m == ms[-1]),
-                    )
-                nc.vector.tensor_copy(h_all[:, ms[0] : ms[-1] + 1, cols], h_acc[:])
+                h_out = h_all[:, ms[0] : ms[-1] + 1, halves[a]]
+                if a == 0 and len(ms) > 1:
+                    nc.scalar.activation(out=h_out, in_=h_acc[:], func=ACT.Copy)
+                else:
+                    nc.vector.tensor_copy(h_out, h_acc[:])
                 for m in ms:
                     nc.scalar.activation(
-                        out=ds_rows[m][:].indirect(half_of(n3_list, a)), in_=h_all[:, m, cols], func=ACT.Copy
+                        out=ds_rows[m][:].indirect(half_of(n3_list, a)), in_=h_all[:, m, halves[a]], func=ACT.Copy
                     )
+
+        last = PACK - 1
+        for a in range(2):
+            for t in range(PACK):
+                fetch(a, t)
+        for t in range(PACK):
+            subtract(0, t)
+            if t > 0:
+                join(0, t - 1)
+            weigh(0, t)
+        subtract(1, 0)
+        join(0, last)
+        weigh(1, 0)
+        weave(0)
+        subtract(1, 1)
+        quantise(0)
+        send(0, multiply(0))
+        join(1, 0)
+        weigh(1, 1)
+        for t in range(2, PACK):
+            subtract(1, t)
+            join(1, t - 1)
+            weigh(1, t)
+        join(1, last)
+        weave(1)
+        quantise(1)
+        send(1, multiply(1))
 
         for m in range(N // P):
             res = keep.tile([P, S], F32, name=f"res{m}")

from contextlib import ExitStack

import concourse.mybir as mybir

K, T, S, N, G, H = 512, 1024, 256, 512, 2048, 512
FLOPS = 2 * K * H * S + 2 * H * N * S + 2 * K * N * S

F32 = mybir.dt.float32
BF16 = mybir.dt.bfloat16
I32 = mybir.dt.int32
U32 = mybir.dt.uint32
U16 = mybir.dt.uint16
U8 = mybir.dt.uint8
FP8X4 = mybir.dt.float8_e4m3fn_x4
ALU = mybir.AluOpType
ACT = mybir.ActivationFunctionType

P = 128
PACK = 4
QUADS = 4
HALF = S // 2
LIST_COLS = HALF // 16
HALF_BYTES = 4 * HALF
D_FIRST, X_FIRST, W2_FIRST, W1_FIRST = 0, 4, 8, 12
OUT_GROUPS = (range(0, 1), range(1, N // P))


def load_words(queue, tile, words):
    queue.dma_start(out=tile[:].bitcast(I32), in_=words[0].rearrange("p n r -> p (n r)").bitcast(I32))


def load_scale_rows(queue, plane, scales, first, q):
    queue.dma_start(
        out=plane[32 * q + first : 32 * q + first + 4, :].bitcast(I32),
        in_=scales[0, 4 * q : 4 * q + 4, :].bitcast(I32),
    )


def load_column(queue, tile, vec):
    queue.dma_start(out=tile[:], in_=vec.rearrange("(p t) o -> p (t o)", t=PACK))


def tile_picked_dwmeblsendmx_none_p_kernel(
    tc, x_words, x_scales, d_words, d_scales, sl, th, gn, w1_words, w1_scales, w2_words, w2_scales,
    offs, ci, n1, n2, two, n3, out,
):
    nc = tc.nc
    with ExitStack() as ctx:
        lists = ctx.enter_context(tc.tile_pool(name="lists", bufs=1))
        keep = ctx.enter_context(tc.tile_pool(name="keep", bufs=1))
        on_d = ctx.enter_context(tc.tile_pool(name="on_d", bufs=1))
        on_x = ctx.enter_context(tc.tile_pool(name="on_x", bufs=1))
        on_z = ctx.enter_context(tc.tile_pool(name="on_z", bufs=1))
        psum = ctx.enter_context(tc.psum_pool(name="psum", bufs=1))

        def load_list(name, src):
            tile = lists.tile([P, src.shape[1]], U16, name=name + "_list")
            nc.sync.dma_start(tile[:], src)
            return tile

        def half_of(list_tile, a):
            return list_tile[:, a * LIST_COLS : (a + 1) * LIST_COLS]

        d_plane = keep.tile([P, G], U8, name="d_plane", align_bytes=64)
        x_plane = keep.tile([P, T], U8, name="x_plane", align_bytes=64)
        w_plane = keep.tile([P, N], U8, name="w_plane", align_bytes=64)
        d_table = on_d.tile([P, G], U32, name="d_table", align_bytes=64, offset=0)
        x_table = on_x.tile([P, T], U32, name="x_table", align_bytes=64, offset=0)
        w1_codes = keep.tile([P, N], U32, name="w1_codes", align_bytes=64)
        w2_codes = keep.tile([P, N], U32, name="w2_codes", align_bytes=64)
        slope = keep.tile([P, PACK], F32, name="slope")
        thresh = keep.tile([P, PACK], F32, name="thresh")
        gain = keep.tile([P, PACK], F32, name="gain")

        nc.vector.memset(d_plane[:, : G // 2].bitcast(I32), 0)
        nc.gpsimd.memset(d_plane[:, G // 2 :].bitcast(I32), 0)
        nc.vector.memset(x_plane[:].bitcast(I32), 0)
        nc.gpsimd.memset(w_plane[:].bitcast(I32), 0)

        ci_list = load_list("ci", ci)
        offs_list = load_list("offs", offs)
        for q in range(QUADS):
            load_scale_rows(nc.scalar if q < QUADS // 2 else nc.sync, d_plane, d_scales, D_FIRST, q)
        load_words(nc.sync, d_table, d_words)
        for q in range(QUADS):
            load_scale_rows(nc.scalar if q < QUADS - 1 else nc.gpsimd, x_plane, x_scales, X_FIRST, q)
        n1_list = load_list("n1", n1)
        n2_list = load_list("n2", n2)
        load_words(nc.sync, x_table, x_words)
        two_list = load_list("two", two)
        load_words(nc.sync, w2_codes, w2_words)
        load_words(nc.sync, w1_codes, w1_words)
        for tile, vec in ((thresh, th), (slope, sl), (gain, gn)):
            load_column(nc.gpsimd, tile, vec)
        for q in range(QUADS):
            load_scale_rows(nc.sync, w_plane, w2_scales, W2_FIRST, q)
            load_scale_rows(nc.gpsimd if q < QUADS - 1 else nc.sync, w_plane, w1_scales, W1_FIRST, q)
        n3_list = load_list("n3", n3)

        minus_thresh = keep.tile([P, PACK], F32, name="minus_thresh")
        nc.scalar.activation(out=minus_thresh[:], in_=thresh[:], func=ACT.Copy, scale=-1.0)

        d_codes = keep.tile([P, H], U32, name="d_codes", align_bytes=64)
        d_bytes = keep.tile([P, H], U8, name="d_bytes", align_bytes=64)
        nc.vector.tensor_copy(d_bytes[:].rearrange("p (t m) -> p m t", t=PACK), d_plane[:].indirect(ci_list[:]))
        nc.vector.tensor_copy(d_codes[:].rearrange("p (t m) -> p m t", t=PACK), d_table[:].indirect(ci_list[:]))
        xq_codes = on_d.tile([P, S], U32, name="xq_codes", align_bytes=64, offset=0)
        xq_bytes = on_d.tile([P, S], U8, name="xq_bytes", align_bytes=64, offset=4 * S)
        two_bytes = on_d.tile([P, S], U8, name="two_bytes", align_bytes=64, offset=5 * S)
        bias = on_d.tile([P, PACK], F32, name="bias", align_bytes=64, offset=6 * S)
        nc.vector.tensor_copy(xq_codes[:], x_table[:].indirect(offs_list[:]))
        nc.vector.tensor_copy(xq_bytes[:], x_plane[:].indirect(offs_list[:]))
        nc.vector.tensor_tensor(bias[:], slope[:], minus_thresh[:], ALU.mult)
        nc.vector.tensor_copy(two_bytes[:], x_plane[:].indirect(two_list[:]))

        s_rows = []
        for t in range(PACK):
            cols = slice(P * t, P * (t + 1))
            s_acc = psum.tile([P, S], F32, name=f"s_acc{t}")
            nc.tensor.matmul_mx(
                out=s_acc[:], lhsT=d_codes[:, cols].bitcast(FP8X4), lhsT_scale=d_bytes[D_FIRST:, cols],
                rhs=xq_codes[:].bitcast(FP8X4), rhs_scale=xq_bytes[X_FIRST:, :], start=True, stop=True,
            )
            s_row = keep.tile([P, S], F32, name=f"s{t}")
            if t == 0:
                nc.scalar.activation(out=s_row[:], in_=s_acc[:], func=ACT.Copy, scale=0.0625)
            else:
                nc.vector.tensor_scalar(s_row[:], s_acc[:], 0.0625, None, ALU.mult)
            s_rows.append(s_row)

        two_codes = keep.tile([P, S], U32, name="two_codes", tag="d_codes", align_bytes=64)
        nc.vector.tensor_copy(two_codes[:], x_table[:].indirect(two_list[:]))

        h_all = keep.tile([P, N // P, S], F32, name="h_all")
        ds_rows = [keep.tile([P, S], F32, name=f"ds{m}") for m in range(N // P)]

        halves = [slice(a * HALF, (a + 1) * HALF) for a in range(2)]

        z_rows = [
            on_z.tile([P, PACK, HALF], BF16, name="z_rows0", align_bytes=64, offset=0),
            keep.tile([P, PACK, HALF], BF16, name="z_rows1", align_bytes=64),
        ]
        z_woven = [
            on_z.tile([P, HALF, PACK], BF16, name="z_woven0", align_bytes=64, offset=2 * HALF_BYTES),
            keep.tile([P, HALF, PACK], BF16, name="z_woven1", align_bytes=64),
        ]
        z_codes = [
            on_z.tile([P, HALF], U32, name="z_codes0", align_bytes=64, offset=4 * HALF_BYTES),
            keep.tile([P, HALF], U32, name="z_codes1", align_bytes=64),
        ]
        z_bytes = [keep.tile([P, HALF], U8, name=f"z_bytes{a}", align_bytes=64) for a in range(2)]
        pa, sg, diff, step = {}, {}, {}, {}

        def fetch(a, t):
            if a == 0:
                pa[a, t] = keep.tile([P, HALF], F32, name=f"pa0{t}")
                sg[a, t] = keep.tile([P, HALF], F32, name=f"sg0{t}")
            else:
                pa[a, t] = on_x.tile([P, HALF], F32, name=f"pa1{t}", offset=2 * t * HALF_BYTES)
                sg[a, t] = on_x.tile([P, HALF], F32, name=f"sg1{t}", offset=(2 * t + 1) * HALF_BYTES)
            nc.scalar.activation(out=pa[a, t][:], in_=s_rows[t][:].indirect(half_of(n1_list, a)), func=ACT.Copy)
            nc.scalar.activation(
                out=sg[a, t][:], in_=s_rows[t][:].indirect(half_of(n2_list, a)), func=ACT.Sigmoid,
                scale=slope[:, t : t + 1], bias=bias[:, t : t + 1],
            )

        def subtract(a, t):
            if a == 0:
                diff[a, t] = keep.tile([P, HALF], F32, name=f"diff0{t}")
            elif t == 0:
                diff[a, t] = keep.tile([P, HALF], F32, name="diff10", tag=f"diff0{PACK - 1}")
            else:
                diff[a, t] = on_z.tile([P, HALF], F32, name=f"diff1{t}", offset=2 * (t - 1) * HALF_BYTES)
            nc.vector.tensor_tensor(diff[a, t][:], s_rows[t][:, halves[a]], pa[a, t][:], ALU.subtract)

        def weigh(a, t):
            step[a, t] = keep.tile([P, HALF], F32, name=f"step{a}{t}")
            nc.vector.scalar_tensor_tensor(
                step[a, t][:], diff[a, t][:], gain[:, t : t + 1], sg[a, t][:], ALU.mult, ALU.mult
            )

        def join(a, t):
            nc.vector.scalar_tensor_tensor(
                z_rows[a][:, t, :], pa[a, t][:], gain[:, t : t + 1], step[a, t][:], ALU.mult, ALU.add
            )

        def weave(a):
            nc.vector.tensor_copy(
                z_woven[a][:].rearrange("p (c i) t -> p c t i", i=4),
                z_rows[a][:].rearrange("p t (c i) -> p c t i", i=4),
            )

        def quantise(a):
            nc.vector.quantize_mx(
                out=z_codes[a][:].bitcast(FP8X4), scales=z_bytes[a][:],
                in_=z_woven[a][:].rearrange("p j t -> p (j t)"),
            )

        def multiply(a):
            h_accs = [psum.tile([P, len(ms), HALF], F32, name=f"h_acc{a}{ms[0]}") for ms in OUT_GROUPS]
            operands = (
                (w2_codes, W2_FIRST, two_codes[:, halves[a]], two_bytes[X_FIRST:, halves[a]]),
                (w1_codes, W1_FIRST, z_codes[a][:], z_bytes[a][:]),
            )
            for k, (w_codes, w_first, codes, scale_bytes) in enumerate(operands):
                for h_acc, ms in zip(h_accs, OUT_GROUPS):
                    for m in ms:
                        rows = slice(P * m, P * (m + 1))
                        nc.tensor.matmul_mx(
                            out=h_acc[:, m - ms[0], :],
                            lhsT=w_codes[:, rows].bitcast(FP8X4), lhsT_scale=w_plane[w_first:, rows],
                            rhs=codes.bitcast(FP8X4), rhs_scale=scale_bytes,
                            start=(k == 0 and m == ms[0]), stop=(k == 1 and m == ms[-1]),
                        )
            return h_accs

        def send(a, h_accs):
            for h_acc, ms in zip(h_accs, OUT_GROUPS):
                h_out = h_all[:, ms[0] : ms[-1] + 1, halves[a]]
                if a == 0 and len(ms) > 1:
                    nc.scalar.activation(out=h_out, in_=h_acc[:], func=ACT.Copy)
                else:
                    nc.vector.tensor_copy(h_out, h_acc[:])
                for m in ms:
                    nc.scalar.activation(
                        out=ds_rows[m][:].indirect(half_of(n3_list, a)), in_=h_all[:, m, halves[a]], func=ACT.Copy
                    )

        last = PACK - 1
        for a in range(2):
            for t in range(PACK):
                fetch(a, t)
        for t in range(PACK):
            subtract(0, t)
            if t > 0:
                join(0, t - 1)
            weigh(0, t)
        subtract(1, 0)
        join(0, last)
        weigh(1, 0)
        weave(0)
        subtract(1, 1)
        quantise(0)
        send(0, multiply(0))
        join(1, 0)
        weigh(1, 1)
        for t in range(2, PACK):
            subtract(1, t)
            join(1, t - 1)
            weigh(1, t)
        join(1, last)
        weave(1)
        quantise(1)
        send(1, multiply(1))

        for m in range(N // P):
            res = keep.tile([P, S], F32, name=f"res{m}")
            nc.vector.tensor_tensor(res[:], h_all[:, m, :], ds_rows[m][:], ALU.subtract)
            nc.sync.dma_start(out=out[P * m : P * (m + 1), :], in_=res[:])
